import numpy as np
import ml_dtypes


def mxq(x, axis, fmt="e4m3"):
    dtype, down = {"e4m3": (ml_dtypes.float8_e4m3fn, 7), "e5m2": (ml_dtypes.float8_e5m2, 14)}[fmt]
    v = np.moveaxis(np.asarray(x, np.float32).astype(ml_dtypes.bfloat16).astype(np.float64), axis, -1)
    blocks = v.reshape(v.shape[:-1] + (-1, 32))
    amax = np.abs(blocks).max(-1, keepdims=True)
    byte = np.maximum(np.where(amax > 0, np.frexp(amax)[1] - 1 + 127, 0) - down, 1)
    scale = np.exp2(byte - 127.0)
    codes = (blocks / scale).astype(np.float32).astype(dtype).astype(np.float64)
    return np.moveaxis((codes * scale).reshape(v.shape), -1, axis)


WIDE = False


def mx_kscale(k):
    if not WIDE:
        return np.ones(k)
    levels = np.array([10, -10, 5, -5, 0])
    if k % 512:
        return np.exp2(np.random.permutation(np.resize(levels, k // 32))).repeat(32)
    a = np.empty((k // 512, 16))
    for p in range(k // 512):
        a[p, :8] = np.random.permutation(np.resize(levels, 8))
        for g in range(8):
            far = levels[np.abs(levels - a[p, g]) >= 10]
            a[p, g + 8] = far[np.random.randint(len(far))]
    return np.exp2(a.ravel()).repeat(32)


BF16 = ml_dtypes.bfloat16


def bf(x):
    return np.asarray(x, np.float32).astype(BF16)


def f64(x):
    return np.asarray(x).astype(np.float64)


E2M1 = np.array([0.0, 0.5, 1.0, 1.5, 2.0, 3.0, 4.0, 6.0, -0.0, -0.5, -1.0, -1.5, -2.0, -3.0, -4.0, -6.0])


def pack_weight(w, fmt):
    k, n = w.shape
    w = f64(bf(w)).reshape(k // 32, 32, n)
    amax = np.abs(w).max(1)
    if fmt == "e4m3":
        byte = np.frexp(amax)[1] - 1 + 127 - 7
    else:
        mant, ex = np.frexp(amax / 6.0)
        byte = np.where(mant > 0.5, ex, ex - 1) + 127
    byte = np.clip(np.where(amax > 0, byte, 1), 1, 254)
    scaled = (w * np.exp2(127.0 - byte)[:, None, :]).reshape(k, n).astype(np.float32)
    by_word = np.ascontiguousarray(scaled.reshape(k // 512, 128, 4, n).transpose(0, 1, 3, 2))
    if fmt == "e4m3":
        words = by_word.astype(ml_dtypes.float8_e4m3fn).view(np.uint8)
    else:
        c = by_word.astype(ml_dtypes.float4_e2m1fn).view(np.uint8) & 0xF
        words = c[..., 0::2] | (c[..., 1::2] << 4)
    return np.ascontiguousarray(words), np.ascontiguousarray(byte.astype(np.uint8).reshape(k // 512, 16, n))


def unpack_weight(words, scales, fmt):
    g, p, n, _ = words.shape
    if fmt == "e4m3":
        vals = np.ascontiguousarray(words).view(ml_dtypes.float8_e4m3fn).astype(np.float64)
    else:
        nib = np.empty((g, p, n, 4), np.uint8)
        nib[..., 0::2] = words & 0xF
        nib[..., 1::2] = words >> 4
        vals = E2M1[nib]
    vals = vals * np.repeat(np.exp2(scales.astype(np.float64) - 127.0), 8, axis=1)[..., None]
    return vals.transpose(0, 1, 3, 2).reshape(g * 512, n)
def pack4(w):
    words, scales = pack_weight(w, "e2m1")
    return words.reshape(words.shape[0], 128, -1), scales


def unpack4(words, scales):
    return unpack_weight(words.reshape(words.shape[0], 128, -1, 2), scales, "e2m1")


M, S, E, A = 1024, 1536, 512, 1024


def draw0():
    s = mx_kscale(S)
    r = mx_kscale(E)
    t = mx_kscale(A)
    F = np.random.standard_normal((S, A)) / np.sqrt(S) / s[:, None] * t
    L = np.random.standard_normal((E, A)) / np.sqrt(E) / r[:, None] * t
    B = np.random.standard_normal((A, S)) / np.sqrt(A) / t[:, None]
    L_words, L_scales = pack4(L)
    B_words, B_scales = pack4(B)
    return {"x": bf(np.random.standard_normal((M, S)) * s),
            "e": bf(np.random.standard_normal((M, E)) * r),
            "F": bf(F),
            "L_words": L_words, "L_scales": L_scales,
            "lo": bf(-(1 + np.random.random(A)) * t),
            "hi": bf((1 + np.random.random(A)) * t),
            "B_words": B_words, "B_scales": B_scales,
            "drift": bf(np.random.standard_normal((M, S)))}


def core(x, e, F, L_words, L_scales, lo, hi, B_words, B_scales, drift):
    fb = mxq(f64(x), 1, "e4m3") @ mxq(f64(F), 0, "e4m3")
    ia = mxq(f64(e), 1, "e4m3") @ unpack4(L_words, L_scales)
    u = fb + ia
    u = np.maximum(np.minimum(u, f64(hi)), f64(lo))
    return (mxq(u, 1, "e4m3") @ unpack4(B_words, B_scales)) + f64(drift)


def e4m3fn_bytes(y):
    return np.clip(np.asarray(y, np.float64), -448.0, 448.0).astype(np.float32).astype(ml_dtypes.float8_e4m3fn).view(np.uint8)


def e4m3fn_values(b):
    return np.asarray(b, np.uint8).view(ml_dtypes.float8_e4m3fn).astype(np.float64)


def setup_inputs():
    d = draw0()
    x0 = np.asarray(d['x']).astype(np.float64)
    s = (np.max(np.abs(x0), axis=(0,), keepdims=True) / 448.0).astype(np.float32)
    out = {}
    for k, v in d.items():
        if k == 'x':
            out['x_bytes'] = e4m3fn_bytes(x0 / s.astype(np.float64))
            out['x_scale'] = s
        else:
            out[k] = v
    return out


def reference(x_bytes, x_scale, e, F, L_words, L_scales, lo, hi, B_words, B_scales, drift):
    return core(e4m3fn_values(x_bytes) * x_scale.astype(np.float64), e, F, L_words, L_scales, lo, hi, B_words, B_scales, drift)

from contextlib import ExitStack

import concourse.mybir as mybir
from concourse.masks import make_identity

M, S, E, A = 1024, 1536, 512, 1024
FLOPS = 2 * M * A * (S + E) + 2 * M * A * S

F32 = mybir.dt.float32
BF16 = mybir.dt.bfloat16
U32 = mybir.dt.uint32
I32 = mybir.dt.int32
U8 = mybir.dt.uint8
FP8 = mybir.dt.float8_e4m3fn
FP8X4 = mybir.dt.float8_e4m3fn_x4
FP4X4 = mybir.dt.float4_e2m1fn_x4
ALU = mybir.AluOpType
P = 128
SCRIPT = """
LW:0 LW:1 X:1 X:0 FI:0,0 XT:0,0 XT:0,3 FI:1,0 XT:0,1 FI:2,0 XE:0,1 XE:0,0 XT:0,2 X:2
LM: X:3 XE:0,2 LS:0 FQ:2,0 FQ:1,0 FQ:0,0 XT:1,2 XE:0,3 XT:1,0 X:5 LS:1 XQ:0,0 XE:1,2
XT:1,3 FI:0,1 XE:1,3 XT:1,1 X:4 XE:1,1 XE:1,0 XQ:1,3 XQ:0,3 XQ:0,2 XQ:1,1 XT:2,0 XQ:1,0 FI:2,1
FI:1,1 XQ:0,1 XQ:1,2 XT:2,1 XE:2,1 XT:2,2 XE:2,0 X:6 S1:0,0,0 X:7 S1:0,0,3 S1:0,0,2 S1:0,0,1 FQ:0,1
XQ:2,1 UE:0,0,2 UE:0,0,0 XT:3,0 UE:0,0,3 XT:3,2 XE:2,2 FQ:1,1 FQ:2,1 XQ:2,0 XT:2,3 XE:3,0 UC:0,0,3 UE:0,0,1
S1:0,1,0 UC:0,0,0 XE:2,3 XQ:2,2 XQ:3,0 S1:0,1,1 UE:0,1,0 UC:0,0,2 XT:3,3 XE:3,2 S1:0,1,2 XT:3,1 UC:0,0,1 UE:0,1,1
XE:3,1 XQ:3,2 XQ:2,3 UC:0,1,0 XE:3,3 XQ:3,1 UC:0,1,1 UE:0,1,2 S1:0,1,3 XQ:3,3 S1:1,0,2 UE:0,1,3 UE:1,0,2 UI:0,0,0
S1:1,0,1 S1:1,1,2 UC:0,1,2 UC:0,1,3 S1:1,1,0 UI:0,0,1 S1:1,0,0 UI:0,1,0 UI:0,1,1 UE:1,0,1 UE:1,1,2 UQ:0,1,0 UQ:0,0,0 S2:1,0
S2:0,1 UE:1,0,0 AD:0,1 S2:0,2 UE:1,1,0 S1:1,0,3 SE:0,2 S1:1,1,1 AD:0,2 S2:0,0 S1:1,1,3 AD:1,0 UE:1,0,3 UC:1,1,2
UC:1,0,1 UC:1,1,0 UE:1,1,1 S2:1,1 UQ:0,0,1 UQ:0,1,1 UC:1,0,3 UC:1,0,0 AD:0,0 UC:1,0,2 UE:1,1,3 UI:1,0,1 UC:1,1,1 S2:2,0
UC:1,1,3 S2:1,2 UI:1,0,0 AD:1,1 SE:1,2 AD:1,2 AD:2,0 UQ:1,0,0 S2:2,1 AD:2,1 UI:1,1,0 S2:2,2 S2:3,0 SE:2,2
S2:3,2 UQ:1,0,1 SE:3,2 UQ:1,1,0 S2:4,2 S2:5,0 AD:3,0 UI:1,1,1 AD:2,2 UQ:1,1,1 S2:5,2 SE:4,2 AD:4,2 AD:5,0
S2:3,1 SE:5,2 S2:4,1 S2:4,0 AD:3,1 S2:5,1 S2:6,2 AD:4,1 AD:3,2 S2:6,0 AD:4,0 AD:5,1 S2:7,2 S2:7,0
AD:5,2 AD:6,0 AD:7,0 SE:6,2 SE:7,2 S2:7,1 S2:6,1 AD:6,2 AD:7,2 AD:7,1 AD:6,1
"""
VF = ()
UIV = 1
GP = ((0, 2), (1, 2), (2, 2), (3, 2), (4, 2), (5, 2), (6, 2), (7, 2),)


def tile_clipped_feedback_control_s3_kernel(
    tc, x_bytes, x_scale, e, F, L_words, L_scales, lo, hi, B_words, B_scales, drift, out
):
    nc = tc.nc
    with ExitStack() as ctx:
        keep = ctx.enter_context(tc.tile_pool(name="keep", bufs=1))
        stage = ctx.enter_context(tc.tile_pool(name="stage", bufs=4))
        psa = ctx.enter_context(tc.psum_pool(name="psa", bufs=4))
        psb = ctx.enter_context(tc.psum_pool(name="psb", bufs=4))

        ident = keep.tile([P, P], F32, name="ident")
        make_identity(nc, ident[:])
        lim_bf = [keep.tile([P, 2, 4], BF16, name=f"lim_bf{k}") for k in range(2)]
        nc.gpsimd.dma_start(out=lim_bf[0][:], in_=hi.rearrange("(g p t) -> p g t", p=P, t=4))
        nc.gpsimd.dma_start(out=lim_bf[1][:], in_=lo.rearrange("(g p t) -> p g t", p=P, t=4))
        l_plane = keep.tile([P, A], U8, name="l_plane", align_bytes=64)
        b_plane = keep.tile([P, 2, S], U8, name="b_plane", align_bytes=64)
        nc.vector.memset(l_plane[:].bitcast(I32), 0)
        nc.vector.memset(b_plane[:].rearrange("p g n -> p (g n)").bitcast(I32), 0)

        l_raw = keep.tile([P, 2 * A], U8, name="l_raw")
        scale_bc = keep.tile([P, S], F32, name="scale_bc")
        xb = [keep.tile([P, 2, S], U8, name=f"xb{j}") for j in range(4)]
        eb = [keep.tile([P, 4, E], BF16, name=f"eb{h}") for h in range(2)]
        fr = [[keep.tile([P, 4, 512], BF16, name=f"fr{c}{g}") for g in range(2)] for c in range(3)]
        bw = keep.tile([P, 2, 2 * S], U8, name="bw", align_bytes=64)
        dr = [keep.tile([P, S], BF16, name=f"dr{i}") for i in range(8)]

        def ld_x(j):
            nc.sync.dma_start(out=xb[j][:], in_=x_bytes[256 * j:256 * j + 256, :].rearrange("(i p) k -> p i k", p=P))

        def ld_e(h):
            nc.sync.dma_start(out=eb[h][:], in_=e[512 * h:512 * h + 512, :].rearrange("(i p) k -> p i k", p=P))

        def ld_f(c, g):
            nc.sync.dma_start(
                out=fr[c][g][:],
                in_=F[512 * c:512 * c + 512, 512 * g:512 * g + 512].rearrange("(p j) a -> p j a", j=4),
            )

        nc.sync.dma_start(out=l_raw[:], in_=L_words[0])
        ld_f(0, 0)
        ld_x(0)
        nc.sync.dma_start(out=scale_bc[:], in_=x_scale.rearrange("o k -> (o k)").partition_broadcast(P))
        for q in range(4):
            nc.sync.dma_start(
                out=l_plane[32 * q:32 * q + 4, :].bitcast(I32), in_=L_scales[0, 4 * q:4 * q + 4, :].bitcast(I32)
            )
        ld_f(1, 0)
        ld_x(1)
        ld_f(2, 0)
        ld_e(0)
        ld_f(0, 1)
        ld_x(2)
        ld_f(1, 1)
        ld_x(3)
        ld_f(2, 1)
        ld_e(1)
        nc.sync.dma_start(out=bw[:], in_=B_words.rearrange("g p n -> p g n"))
        for q in range(4):
            nc.sync.dma_start(
                out=b_plane[32 * q:32 * q + 4, :, :].bitcast(I32),
                in_=B_scales[:, 4 * q:4 * q + 4, :].rearrange("g q n -> q g n").bitcast(I32),
            )
        for i in range(8):
            nc.sync.dma_start(out=dr[i][:], in_=drift[128 * i:128 * i + 128, :])

        lim = keep.tile([P, 2, 2, 4], F32, name="lim")
        lw = keep.tile([P, 2, 4, 256], U8, name="lw", align_bytes=64)
        ls = keep.tile([P, 2, 4, P], U8, name="ls", align_bytes=64)
        fq = [[keep.tile([P, 512], U32, name=f"fq{c}{g}", align_bytes=64) for g in range(2)] for c in range(3)]
        fs = [[keep.tile([P, 512], U8, name=f"fs{c}{g}", align_bytes=64) for g in range(2)] for c in range(3)]
        xq = [[keep.tile([P, 512], U32, name=f"xq{h}{c}", align_bytes=64) for c in range(4)] for h in range(2)]
        xsc = [[keep.tile([P, 512], U8, name=f"xsc{h}{c}", align_bytes=64) for c in range(4)] for h in range(2)]
        uq = [[keep.tile([P, 512], U32, name=f"uq{h}{g}", align_bytes=64) for g in range(2)] for h in range(2)]
        us = [[keep.tile([P, 512], U8, name=f"us{h}{g}", align_bytes=64) for g in range(2)] for h in range(2)]
        live = {}

        def LW(g):
            nc.vector.tensor_copy(
                out=lw[:, g].rearrange("p t (m b) -> p t m b", b=2),
                in_=l_raw[:, 1024 * g:1024 * g + 1024].rearrange("p (m t b) -> p t m b", t=4, b=2),
            )

        def LS(g):
            nc.vector.tensor_copy(
                out=ls[:, g], in_=l_plane[:, 512 * g:512 * g + 512].rearrange("p (m t) -> p t m", t=4)
            )

        def LM():
            for k in range(2):
                nc.vector.tensor_copy(out=lim[:, k], in_=lim_bf[k][:])

        def X(i):
            j = i // 2
            xs = stage.tile([P, S], BF16, name=f"xs{i}", tag="xs", bufs=4)
            live["xs", i] = xs
            nc.vector.tensor_tensor(out=xs[:], in0=xb[j][:, i % 2, :].bitcast(FP8), in1=scale_bc[:], op=ALU.mult)

        def XT(j, c):
            bank = psb.tile([P, 2, 2, P], F32, name=f"xt{j}{c}", tag="b")
            live["xt", j, c] = bank
            for i in range(2):
                src = live["xs", 2 * j + i][:] if c < 3 else eb[j // 2][:, 2 * (j % 2) + i, :]
                words = src.bitcast(F32)
                base = 256 * c if c < 3 else 0
                for u in range(2):
                    nc.tensor.transpose(bank[:, i, u, :], words[:, base + u:base + 256:2], ident[:])

        def XE(j, c):
            grp = stage.tile([P, 256, 4], BF16, name=f"xg{j}{c}", tag="xg", bufs=8, align_bytes=64)
            live["xg", j, c] = grp
            bank = live["xt", j, c]
            nc.scalar.copy(
                out=grp[:].bitcast(F32).rearrange("p (i r) u -> p i r u", i=2),
                in_=bank[:].rearrange("p i u r -> p i r u"),
            )

        def XQ(j, c):
            h, o = j // 2, 256 * (j % 2)
            nc.vector.quantize_mx(
                out=xq[h][c][:, o:o + 256].bitcast(FP8X4),
                scales=xsc[h][c][:, o:o + 256],
                in_=live["xg", j, c][:].rearrange("p m t -> p (m t)"),
            )

        def FI(c, g):
            fg = stage.tile([P, 4, P, 4], BF16, name=f"fg{c}{g}", tag="fg", bufs=3, align_bytes=64)
            live["fg", c, g] = fg
            src = fr[c][g][:].rearrange("p j (m t) -> p t m j", t=4)
            if (c, g) in VF:
                nc.vector.tensor_copy(out=fg[:], in_=src)
            else:
                nc.scalar.copy(out=fg[:], in_=src)

        def FQ(c, g):
            nc.vector.quantize_mx(
                out=fq[c][g][:].bitcast(FP8X4),
                scales=fs[c][g][:],
                in_=live["fg", c, g][:].rearrange("p t m j -> p (t m j)"),
            )

        def S1(h, g, t):
            acc = psa.tile([P, 512], F32, name=f"acc{h}{g}{t}", tag="a")
            live["acc", h, g, t] = acc
            cols = slice(128 * t, 128 * t + 128)
            for c in range(4):
                if c < 3:
                    w, ws = fq[c][g][:, cols].bitcast(FP8X4), fs[c][g][:, cols]
                else:
                    w, ws = lw[:, g, t, :].bitcast(FP4X4), ls[:, g, t, :]
                nc.tensor.matmul_mx(
                    out=acc[:], lhsT=w, lhsT_scale=ws,
                    rhs=xq[h][c][:].bitcast(FP8X4), rhs_scale=xsc[h][c][:],
                    start=(c == 0), stop=(c == 3),
                )

        def UE(h, g, t):
            if ("up", h, g) not in live:
                live["up", h, g] = stage.tile([P, 4, 512], BF16, name=f"up{h}{g}", tag="up", bufs=3)
            nc.scalar.copy(out=live["up", h, g][:, t, :], in_=live["acc", h, g, t][:])

        def UC(h, g, t):
            u = live["up", h, g][:, t, :]
            nc.vector.tensor_scalar(
                out=u, in0=u, scalar1=lim[:, 0, g, t:t + 1], scalar2=lim[:, 1, g, t:t + 1], op0=ALU.min, op1=ALU.max
            )

        def UI(h, g, k):
            if ("ug", h, g) not in live:
                live["ug", h, g] = stage.tile([P, 512, 4], BF16, name=f"ug{h}{g}", tag="ug", bufs=2, align_bytes=64)
            m = slice(256 * k, 256 * k + 256)
            src = live["up", h, g][:, :, m].rearrange("p t m -> p m t")
            dst = live["ug", h, g][:, m, :]
            if k >= UIV:
                nc.vector.tensor_copy(out=dst, in_=src)
            else:
                nc.scalar.copy(out=dst, in_=src)

        def UQ(h, g, k):
            m = slice(256 * k, 256 * k + 256)
            nc.vector.quantize_mx(
                out=uq[h][g][:, m].bitcast(FP8X4),
                scales=us[h][g][:, m],
                in_=live["ug", h, g][:, m, :].rearrange("p m t -> p (m t)"),
            )

        def S2(i, n):
            h, cols = i // 4, slice(128 * (i % 4), 128 * (i % 4) + 128)
            acc = psb.tile([P, 512], F32, name=f"y{i}{n}", tag="b")
            live["y", i, n] = acc
            for g in range(2):
                nc.tensor.matmul_mx(
                    out=acc[:],
                    lhsT=uq[h][g][:, cols].bitcast(FP8X4), lhsT_scale=us[h][g][:, cols],
                    rhs=bw[:, g, 1024 * n:1024 * n + 1024].bitcast(FP4X4),
                    rhs_scale=b_plane[:, g, 512 * n:512 * n + 512],
                    start=(g == 0), stop=(g == 1),
                )

        def SE(i, n):
            ye = stage.tile([P, 512], F32, name=f"ye{i}{n}", tag="ye", bufs=3)
            live["ye", i, n] = ye
            nc.scalar.copy(out=ye[:], in_=live["y", i, n][:])

        def AD(i, n):
            cols = slice(512 * n, 512 * n + 512)
            ot = stage.tile([P, 512], F32, name=f"ot{i}{n}", tag="ot", bufs=8)
            if (i, n) in GP:
                nc.gpsimd.tensor_tensor(out=ot[:], in0=live["ye", i, n][:], in1=dr[i][:, cols], op=ALU.add)
            else:
                nc.vector.tensor_tensor(out=ot[:], in0=live["y", i, n][:], in1=dr[i][:, cols], op=ALU.add)
            nc.sync.dma_start(out=out[128 * i:128 * i + 128, cols], in_=ot[:])

        steps = {"LW": LW, "LS": LS, "LM": LM, "X": X, "XT": XT, "XE": XE, "XQ": XQ, "FI": FI, "FQ": FQ, "S1": S1,
                 "UE": UE, "UC": UC, "UI": UI, "UQ": UQ, "S2": S2, "SE": SE, "AD": AD}
        with tc.manual_schedule():
            for tok in SCRIPT.split():
                name, args = tok.split(":")
                steps[name](*[int(d) for d in args.split(",") if d != ""])
